import numpy as np
import ml_dtypes


def mxq(x, axis, fmt="e4m3"):
    dtype, down = {"e4m3": (ml_dtypes.float8_e4m3fn, 7), "e5m2": (ml_dtypes.float8_e5m2, 14)}[fmt]
    v = np.moveaxis(np.asarray(x, np.float32).astype(ml_dtypes.bfloat16).astype(np.float64), axis, -1)
    blocks = v.reshape(v.shape[:-1] + (-1, 32))
    amax = np.abs(blocks).max(-1, keepdims=True)
    byte = np.maximum(np.where(amax > 0, np.frexp(amax)[1] - 1 + 127, 0) - down, 1)
    scale = np.exp2(byte - 127.0)
    codes = (blocks / scale).astype(np.float32).astype(dtype).astype(np.float64)
    return np.moveaxis((codes * scale).reshape(v.shape), -1, axis)


WIDE = False


def mx_kscale(k):
    if not WIDE:
        return np.ones(k)
    levels = np.array([10, -10, 5, -5, 0])
    if k % 512:
        return np.exp2(np.random.permutation(np.resize(levels, k // 32))).repeat(32)
    a = np.empty((k // 512, 16))
    for p in range(k // 512):
        a[p, :8] = np.random.permutation(np.resize(levels, 8))
        for g in range(8):
            far = levels[np.abs(levels - a[p, g]) >= 10]
            a[p, g + 8] = far[np.random.randint(len(far))]
    return np.exp2(a.ravel()).repeat(32)


def f64(x):
    return np.asarray(x).astype(np.float64)


def striped(idx):
    return np.tile(np.asarray(idx).reshape(-1, 16).T, (8, 1)).astype(np.uint16)


def unstriped(offs):
    return offs[:16].T.reshape(-1).astype(np.int64)


E2M1 = np.array([0.0, 0.5, 1.0, 1.5, 2.0, 3.0, 4.0, 6.0, -0.0, -0.5, -1.0, -1.5, -2.0, -3.0, -4.0, -6.0])


def pack_weight(w, fmt):
    k, n = w.shape
    w = f64(np.asarray(w, np.float32).astype(ml_dtypes.bfloat16)).reshape(k // 32, 32, n)
    amax = np.abs(w).max(1)
    if fmt == "e4m3":
        byte = np.frexp(amax)[1] - 1 + 127 - 7
    else:
        mant, ex = np.frexp(amax / 6.0)
        byte = np.where(mant > 0.5, ex, ex - 1) + 127
    byte = np.clip(np.where(amax > 0, byte, 1), 1, 254)
    scaled = (w * np.exp2(127.0 - byte)[:, None, :]).reshape(k, n).astype(np.float32)
    by_word = np.ascontiguousarray(scaled.reshape(k // 512, 128, 4, n).transpose(0, 1, 3, 2))
    if fmt == "e4m3":
        words = by_word.astype(ml_dtypes.float8_e4m3fn).view(np.uint8)
    else:
        c = by_word.astype(ml_dtypes.float4_e2m1fn).view(np.uint8) & 0xF
        words = (c[..., 0::2] | (c[..., 1::2] << 4)).reshape(k // 512, 128, 2 * n)
    return np.ascontiguousarray(words), np.ascontiguousarray(byte.astype(np.uint8).reshape(k // 512, 16, n))


def unpack_weight(words, scales, fmt):
    g, _, n = scales.shape
    words = np.ascontiguousarray(words).reshape(g, 128, n, -1)
    if fmt == "e4m3":
        vals = words.view(ml_dtypes.float8_e4m3fn).astype(np.float64)
    else:
        nib = np.empty((g, 128, n, 4), np.uint8)
        nib[..., 0::2] = words & 0xF
        nib[..., 1::2] = words >> 4
        vals = E2M1[nib]
    vals = vals * np.repeat(np.exp2(scales.astype(np.float64) - 127.0), 8, axis=1)[..., None]
    return vals.transpose(0, 1, 3, 2).reshape(g * 512, n)


def bf(x):
    return np.asarray(x, np.float32).astype(ml_dtypes.bfloat16)


def planes(Y):
    r, m = Y.shape
    b = f64(bf(Y)).reshape(r // 32, 32, m)
    amax = np.abs(b).max(1)
    byte = np.clip(np.where(amax > 0, np.frexp(amax)[1] - 1 + 127 - 7, 1), 1, 254)
    codes = (b * np.exp2(127.0 - byte)[:, None, :]).reshape(r, m).astype(np.float32).astype(ml_dtypes.float8_e4m3fn).view(np.uint8)
    words = codes.reshape(r // 512, 128, 4, m).transpose(0, 1, 3, 2)
    return np.ascontiguousarray(words), np.ascontiguousarray(byte.astype(np.uint8).reshape(r // 512, 16, m))


B, N, T, D, NQ = 1, 512, 2048, 1024, 512


def setup_inputs():
    n = np.random.standard_normal
    idx = np.random.permutation(T)[:B * N]
    s = mx_kscale(D)[:, None]
    kp = pack_weight(n((D, T)) / s, "e2m1")
    return {
        "qT": (n((B, D, NQ)) * s * (1.00 / np.sqrt(D))).astype(np.float32),
        "k_words": np.ascontiguousarray(kp[0].reshape(1, 2, 128, T, 2).transpose(0, 2, 3, 1, 4)).reshape(1, 128, T, 4),
        "k_scales": kp[1],
        "dc": (np.random.uniform(0.1, 1.0, (B, 1, NQ))).astype(np.float32),
        "offs": striped(idx),
    }


def reference(qT, k_words, k_scales, dc, offs):
    idx = unstriped(offs)
    pick = lambda x, which: x[:, which].reshape(x.shape[0], B, -1).transpose(1, 0, 2)
    k = unpack_weight(k_words.reshape(1, 128, T, 2, 2).transpose(0, 3, 1, 2, 4).reshape(2, 128, 2 * T), k_scales, "e2m1")
    kg = pick(k, idx)
    qq = mxq(f64(qT), 1, "e4m3")
    a = kg.transpose(0, 2, 1) @ qq
    y = a * f64(dc)
    Y = y[0]
    words, scales = planes(Y)
    return Y, words, scales

@@ -1,0 +1,185 @@
+from contextlib import ExitStack
+
+import concourse.mybir as mybir
+from concourse.masks import make_identity
+
+F32 = mybir.dt.float32
+BF16 = mybir.dt.bfloat16
+I32 = mybir.dt.int32
+U32 = mybir.dt.uint32
+U16 = mybir.dt.uint16
+U8 = mybir.dt.uint8
+FP8X4 = mybir.dt.float8_e4m3fn_x4
+FP4X4 = mybir.dt.float4_e2m1fn_x4
+MULT = mybir.AluOpType.mult
+
+P = 128
+PACK = 4
+SLOTS, POOL, D, NQ = 512, 2048, 1024, 512
+PASSES = 2
+CHUNK = 128
+CHUNKS = NQ // CHUNK
+FLOPS = 2 * SLOTS * D * NQ
+
+
+def interleave(copy, dst, src):
+    copy(
+        out=dst.rearrange("p (c i) t -> p c t i", i=4),
+        in_=src.rearrange("p t (c i) -> p c t i", i=4),
+    )
+
+
+def tile_attend_plw_decay_topk_kernel(tc, qT, k_words, k_scales, dc, offs, out_0, out_1, out_2):
+    nc = tc.nc
+    with ExitStack() as ctx:
+        sb = ctx.enter_context(tc.tile_pool(name="sb", bufs=1))
+        psum = ctx.enter_context(tc.psum_pool(name="psum", bufs=1))
+
+        offsets = sb.tile([P, SLOTS // 16], U16, name="offsets")
+        nc.sync.dma_start(offsets[:], offs)
+
+        scale_pool = sb.tile([P, POOL], U8, name="scale_pool")
+        nc.sync.dma_start(
+            out=scale_pool[0:32, :].bitcast(I32),
+            in_=k_scales.rearrange("o f t -> f o t").bitcast(I32),
+        )
+        nc.vector.memset(scale_pool[32:64, :].bitcast(I32), 0)
+        nc.vector.memset(scale_pool[64:128, :].bitcast(I32), 0)
+
+        dc_cols = sb.tile([P, PACK], F32, name="dc_cols")
+        nc.sync.dma_start(out=dc_cols[:], in_=dc[0, 0].rearrange("(p m) -> p m", m=PACK))
+
+        word_pool = sb.tile([P, POOL], I32, name="word_pool")
+        nc.sync.dma_start(out=word_pool[:], in_=k_words[0].rearrange("p t b -> p (t b)").bitcast(I32))
+
+        q_rows = qT[0].rearrange("(o p j) q -> o p j q", o=PASSES, j=PACK)
+        raw0 = sb.tile([P, PACK, NQ], F32, name="raw0")
+        nc.sync.dma_start(out=raw0[:], in_=q_rows[0])
+        raw1 = []
+        for n, (a, b) in enumerate(((0, 256), (256, 384), (384, 512))):
+            piece = sb.tile([P, PACK, b - a], F32, name="raw1_%d" % n)
+            nc.sync.dma_start(out=piece[:], in_=q_rows[1][:, :, a:b])
+            for c0 in range(0, b - a, CHUNK):
+                raw1.append(piece[:, :, c0 : c0 + CHUNK])
+
+        key_scales = sb.tile([P, PASSES, SLOTS], U8, name="key_scales", align_bytes=64)
+        nc.vector.memset(key_scales[:].rearrange("p o s -> p (o s)").bitcast(I32), 0)
+
+        ident = sb.tile([P, P], F32, name="ident")
+        make_identity(nc, ident[:])
+        dc_ps = psum.tile([P, PACK, P], F32, name="dc_ps")
+        for m in range(PACK):
+            nc.tensor.transpose(dc_ps[:, m, :], dc_cols[:, m : m + 1].to_broadcast([P, P]), ident[:])
+        dc_rows = sb.tile([P, NQ], F32, name="dc_rows")
+        nc.scalar.copy(
+            out=dc_rows[:].rearrange("p (n m) -> p n m", m=PACK),
+            in_=dc_ps[:].rearrange("p m n -> p n m"),
+        )
+
+        scales_listed = sb.tile([P, SLOTS], U8, name="scales_listed")
+        nc.vector.tensor_copy(scales_listed[:], scale_pool[:].indirect(offsets[:]))
+        scales_dealt = sb.tile([P, SLOTS], U8, name="scales_dealt")
+        nc.vector.tensor_copy(
+            out=scales_dealt[:].rearrange("p (r s) -> p s r", r=PACK),
+            in_=scales_listed[:].rearrange("p (s r) -> p s r", r=PACK),
+        )
+        for quad in range(4):
+            nc.scalar.dma_start(
+                out=key_scales[32 * quad : 32 * quad + 4, :, :].bitcast(I32),
+                in_=scales_dealt[8 * quad : 8 * quad + 8, :].bitcast(I32),
+            )
+
+        words_listed = sb.tile([P, SLOTS], U32, name="words_listed")
+        nc.vector.tensor_copy(words_listed[:], word_pool[:].bitcast(U32).indirect(offsets[:]))
+        key_words = sb.tile([P, PASSES, 2 * SLOTS], U8, name="key_words", align_bytes=64)
+        nc.vector.tensor_copy(
+            out=key_words[:].bitcast(U16).rearrange("p o (r s) -> p o s r", r=PACK),
+            in_=words_listed[:].bitcast(U16).rearrange("p (s r o) -> p o s r", r=PACK, o=PASSES),
+        )
+
+        q_codes = [sb.tile([P, NQ], U32, name="q_codes%d" % o, align_bytes=64) for o in range(PASSES)]
+        q_scales = [sb.tile([P, NQ], U8, name="q_scales%d" % o, align_bytes=64) for o in range(PASSES)]
+
+        def quantize(codes, scales, cols, grouped):
+            nc.vector.quantize_mx(
+                out=codes[:, cols].bitcast(FP8X4),
+                scales=scales[:, cols],
+                in_=grouped[:].rearrange("p c t -> p (c t)"),
+            )
+
+        halves = []
+        for h, copy in enumerate((nc.vector.tensor_copy, nc.scalar.copy)):
+            grouped = sb.tile([P, 256, PACK], BF16, name="q0_bf%d" % h, align_bytes=64)
+            interleave(copy, grouped[:], raw0[:, :, 256 * h : 256 * (h + 1)])
+            halves.append(grouped)
+        for h in range(2):
+            quantize(q_codes[0], q_scales[0], slice(256 * h, 256 * (h + 1)), halves[h])
+
+        y_codes = sb.tile([P, NQ], U32, name="y_codes", align_bytes=64)
+        y_scales = sb.tile([P, NQ], U8, name="y_scales", align_bytes=64)
+        y_rows = out_0.rearrange("(s r) q -> s r q", r=PACK)
+        word_rows = out_1[0].rearrange("p q b -> p (q b)").bitcast(I32)
+
+        acc = [None] * CHUNKS
+        y_tiles = [None] * CHUNKS
+        y_bf = [None] * CHUNKS
+        y_pair = sb.tile([P, PACK, 2 * CHUNK], F32, name="y_pair")
+
+        def scores(c):
+            cols = slice(c * CHUNK, (c + 1) * CHUNK)
+            grouped = sb.tile([P, CHUNK, PACK], BF16, name="q1_bf%d" % c, align_bytes=64)
+            interleave(nc.vector.tensor_copy if c == 0 else nc.scalar.copy, grouped[:], raw1[c])
+            quantize(q_codes[1], q_scales[1], cols, grouped)
+            acc[c] = psum.tile([P, PACK, CHUNK], F32, name="acc%d" % c)
+            for r in range(PACK):
+                for o in range(PASSES):
+                    nc.tensor.matmul_mx(
+                        out=acc[c][:, r, :],
+                        lhsT=key_words[:, o, 2 * P * r : 2 * P * (r + 1)].bitcast(FP4X4),
+                        lhsT_scale=key_scales[:, o, P * r : P * (r + 1)],
+                        rhs=q_codes[o][:, cols].bitcast(FP8X4),
+                        rhs_scale=q_scales[o][:, cols],
+                        start=(o == 0),
+                        stop=(o == PASSES - 1),
+                    )
+
+        def decay(c):
+            cols = slice(c * CHUNK, (c + 1) * CHUNK)
+            if c < 2:
+                y_tiles[c] = y_pair[:, :, cols]
+            else:
+                y_tiles[c] = sb.tile([P, PACK, CHUNK], F32, name="y%d" % c)[:]
+            nc.vector.tensor_tensor(
+                y_tiles[c], acc[c][:], dc_rows[:, cols].unsqueeze(1).to_broadcast([P, PACK, CHUNK]), MULT
+            )
+            if c == 1:
+                nc.sync.dma_start(out=y_rows[:, :, 0 : 2 * CHUNK], in_=y_pair[:])
+            elif c > 1:
+                nc.sync.dma_start(out=y_rows[:, :, cols], in_=y_tiles[c])
+            y_bf[c] = sb.tile([P, CHUNK, PACK], BF16, name="y_bf%d" % c, align_bytes=64)
+            interleave(nc.vector.tensor_copy if c == CHUNKS - 1 else nc.scalar.copy, y_bf[c][:], y_tiles[c])
+
+        def planes(c):
+            quantize(y_codes, y_scales, slice(c * CHUNK, (c + 1) * CHUNK), y_bf[c])
+            if c % 2 == 1:
+                pair = slice((c - 1) * CHUNK, (c + 1) * CHUNK)
+                nc.sync.dma_start(out=word_rows[:, pair], in_=y_codes[:, pair].bitcast(I32))
+
+        scores(0)
+        scores(1)
+        scores(2)
+        decay(0)
+        scores(3)
+        decay(1)
+        planes(0)
+        decay(2)
+        planes(1)
+        decay(3)
+        planes(2)
+        planes(3)
+        for quad in range(4):
+            queue = nc.scalar if quad % 2 else nc.sync
+            queue.dma_start(
+                out=out_2[0, 4 * quad : 4 * quad + 4, :].bitcast(I32),
+                in_=y_scales[32 * quad : 32 * quad + 4, :].bitcast(I32),
+            )

@@ -19,6 +19,7 @@ SLOTS, POOL, D, NQ = 512, 2048, 1024, 512
 PASSES = 2
 CHUNK = 128
 CHUNKS = NQ // CHUNK
+HALF = 2 * CHUNK
 FLOPS = 2 * SLOTS * D * NQ
 
 
@@ -39,7 +40,7 @@ def tile_attend_plw_decay_topk_kernel(tc, qT, k_words, k_scales, dc, offs, out_0
         nc.sync.dma_start(offsets[:], offs)
 
         scale_pool = sb.tile([P, POOL], U8, name="scale_pool")
-        nc.sync.dma_start(
+        nc.scalar.dma_start(
             out=scale_pool[0:32, :].bitcast(I32),
             in_=k_scales.rearrange("o f t -> f o t").bitcast(I32),
         )
@@ -47,27 +48,25 @@ def tile_attend_plw_decay_topk_kernel(tc, qT, k_words, k_scales, dc, offs, out_0
         nc.vector.memset(scale_pool[64:128, :].bitcast(I32), 0)
 
         dc_cols = sb.tile([P, PACK], F32, name="dc_cols")
-        nc.sync.dma_start(out=dc_cols[:], in_=dc[0, 0].rearrange("(p m) -> p m", m=PACK))
+        nc.scalar.dma_start(out=dc_cols[:], in_=dc[0, 0].rearrange("(p m) -> p m", m=PACK))
 
         word_pool = sb.tile([P, POOL], I32, name="word_pool")
         nc.sync.dma_start(out=word_pool[:], in_=k_words[0].rearrange("p t b -> p (t b)").bitcast(I32))
 
         q_rows = qT[0].rearrange("(o p j) q -> o p j q", o=PASSES, j=PACK)
-        raw0 = sb.tile([P, PACK, NQ], F32, name="raw0")
-        nc.sync.dma_start(out=raw0[:], in_=q_rows[0])
-        raw1 = []
-        for n, (a, b) in enumerate(((0, 256), (256, 384), (384, 512))):
-            piece = sb.tile([P, PACK, b - a], F32, name="raw1_%d" % n)
-            nc.sync.dma_start(out=piece[:], in_=q_rows[1][:, :, a:b])
-            for c0 in range(0, b - a, CHUNK):
-                raw1.append(piece[:, :, c0 : c0 + CHUNK])
+        raw = {}
+        for o in range(PASSES):
+            raw[0, o] = sb.tile([P, PACK, HALF], F32, name="raw0%d" % o)[:]
+            nc.sync.dma_start(out=raw[0, o], in_=q_rows[o][:, :, 0:HALF])
 
         key_scales = sb.tile([P, PASSES, SLOTS], U8, name="key_scales", align_bytes=64)
         nc.vector.memset(key_scales[:].rearrange("p o s -> p (o s)").bitcast(I32), 0)
 
         ident = sb.tile([P, P], F32, name="ident")
-        make_identity(nc, ident[:])
-        dc_ps = psum.tile([P, PACK, P], F32, name="dc_ps")
+        ident_bf = sb.tile([P, P], BF16, name="ident_bf")
+        make_identity(nc, ident_bf[:])
+        nc.scalar.copy(out=ident[:], in_=ident_bf[:])
+        dc_ps = psum.tile([P, PACK, P], F32, name="dc_ps", tag="bank7")
         for m in range(PACK):
             nc.tensor.transpose(dc_ps[:, m, :], dc_cols[:, m : m + 1].to_broadcast([P, P]), ident[:])
         dc_rows = sb.tile([P, NQ], F32, name="dc_rows")
@@ -76,7 +75,7 @@ def tile_attend_plw_decay_topk_kernel(tc, qT, k_words, k_scales, dc, offs, out_0
             in_=dc_ps[:].rearrange("p m n -> p n m"),
         )
 
-        scales_listed = sb.tile([P, SLOTS], U8, name="scales_listed")
+        scales_listed = sb.tile([P, SLOTS], U8, name="scales_listed", tag="late")
         nc.vector.tensor_copy(scales_listed[:], scale_pool[:].indirect(offsets[:]))
         scales_dealt = sb.tile([P, SLOTS], U8, name="scales_dealt")
         nc.vector.tensor_copy(
@@ -84,10 +83,15 @@ def tile_attend_plw_decay_topk_kernel(tc, qT, k_words, k_scales, dc, offs, out_0
             in_=scales_listed[:].rearrange("p (s r) -> p s r", r=PACK),
         )
         for quad in range(4):
-            nc.scalar.dma_start(
+            nc.sync.dma_start(
                 out=key_scales[32 * quad : 32 * quad + 4, :, :].bitcast(I32),
                 in_=scales_dealt[8 * quad : 8 * quad + 8, :].bitcast(I32),
             )
+
+        raw_late = sb.tile([P, PASSES, PACK, HALF], F32, name="raw_late", tag="late")
+        for o in range(PASSES):
+            raw[1, o] = raw_late[:, o]
+            nc.sync.dma_start(out=raw[1, o], in_=q_rows[o][:, :, HALF:NQ])
 
         words_listed = sb.tile([P, SLOTS], U32, name="words_listed")
         nc.vector.tensor_copy(words_listed[:], word_pool[:].bitcast(U32).indirect(offsets[:]))
@@ -104,44 +108,53 @@ def tile_attend_plw_decay_topk_kernel(tc, qT, k_words, k_scales, dc, offs, out_0
             nc.vector.quantize_mx(
                 out=codes[:, cols].bitcast(FP8X4),
                 scales=scales[:, cols],
-                in_=grouped[:].rearrange("p c t -> p (c t)"),
+                in_=grouped.rearrange("p c t -> p (c t)"),
             )
-
-        halves = []
-        for h, copy in enumerate((nc.vector.tensor_copy, nc.scalar.copy)):
-            grouped = sb.tile([P, 256, PACK], BF16, name="q0_bf%d" % h, align_bytes=64)
-            interleave(copy, grouped[:], raw0[:, :, 256 * h : 256 * (h + 1)])
-            halves.append(grouped)
-        for h in range(2):
-            quantize(q_codes[0], q_scales[0], slice(256 * h, 256 * (h + 1)), halves[h])
 
         y_codes = sb.tile([P, NQ], U32, name="y_codes", align_bytes=64)
         y_scales = sb.tile([P, NQ], U8, name="y_scales", align_bytes=64)
         y_rows = out_0.rearrange("(s r) q -> s r q", r=PACK)
         word_rows = out_1[0].rearrange("p q b -> p (q b)").bitcast(I32)
 
-        acc = [None] * CHUNKS
+        acc = {}
         y_tiles = [None] * CHUNKS
-        y_bf = [None] * CHUNKS
-        y_pair = sb.tile([P, PACK, 2 * CHUNK], F32, name="y_pair")
+        y_pair = sb.tile([P, PACK, HALF], F32, name="y_pair")
+        y_bf = [sb.tile([P, HALF, PACK], BF16, name="y_bf%d" % h, align_bytes=64) for h in range(2)]
 
-        def scores(c):
+        def one_pass(c, r, o):
             cols = slice(c * CHUNK, (c + 1) * CHUNK)
-            grouped = sb.tile([P, CHUNK, PACK], BF16, name="q1_bf%d" % c, align_bytes=64)
-            interleave(nc.vector.tensor_copy if c == 0 else nc.scalar.copy, grouped[:], raw1[c])
-            quantize(q_codes[1], q_scales[1], cols, grouped)
-            acc[c] = psum.tile([P, PACK, CHUNK], F32, name="acc%d" % c)
-            for r in range(PACK):
-                for o in range(PASSES):
-                    nc.tensor.matmul_mx(
-                        out=acc[c][:, r, :],
-                        lhsT=key_words[:, o, 2 * P * r : 2 * P * (r + 1)].bitcast(FP4X4),
-                        lhsT_scale=key_scales[:, o, P * r : P * (r + 1)],
-                        rhs=q_codes[o][:, cols].bitcast(FP8X4),
-                        rhs_scale=q_scales[o][:, cols],
-                        start=(o == 0),
-                        stop=(o == PASSES - 1),
-                    )
+            nc.tensor.matmul_mx(
+                out=acc[c, r // 2][:, r % 2, :],
+                lhsT=key_words[:, o, 2 * P * r : 2 * P * (r + 1)].bitcast(FP4X4),
+                lhsT_scale=key_scales[:, o, P * r : P * (r + 1)],
+                rhs=q_codes[o][:, cols].bitcast(FP8X4),
+                rhs_scale=q_scales[o][:, cols],
+                start=(o == 0),
+                stop=(o == PASSES - 1),
+            )
+
+        def first_pass(h):
+            grouped = sb.tile([P, HALF, PACK], BF16, name="q0_bf%d" % h, align_bytes=64)
+            interleave(nc.scalar.copy, grouped[:], raw[h, 0])
+            quantize(q_codes[0], q_scales[0], slice(h * HALF, (h + 1) * HALF), grouped[:])
+            for c in (2 * h, 2 * h + 1):
+                for b in range(2):
+                    acc[c, b] = psum.tile([P, 2, CHUNK], F32, name="acc%d%d" % (c, b), tag="bank%d" % (2 * c + b))
+                    one_pass(c, 2 * b, 0)
+
+        def second_pass(h):
+            grouped = []
+            for n, copy in enumerate((nc.vector.tensor_copy, nc.scalar.copy)):
+                g = sb.tile([P, CHUNK, PACK], BF16, name="q1_bf%d%d" % (h, n), align_bytes=64)
+                interleave(copy, g[:], raw[h, 1][:, :, n * CHUNK : (n + 1) * CHUNK])
+                grouped.append(g)
+            for n in range(2):
+                c = 2 * h + n
+                quantize(q_codes[1], q_scales[1], slice(c * CHUNK, (c + 1) * CHUNK), grouped[n][:])
+                for b in range(2):
+                    one_pass(c, 2 * b, 1)
+                    one_pass(c, 2 * b + 1, 0)
+                    one_pass(c, 2 * b + 1, 1)
 
         def decay(c):
             cols = slice(c * CHUNK, (c + 1) * CHUNK)
@@ -149,34 +162,41 @@ def tile_attend_plw_decay_topk_kernel(tc, qT, k_words, k_scales, dc, offs, out_0
                 y_tiles[c] = y_pair[:, :, cols]
             else:
                 y_tiles[c] = sb.tile([P, PACK, CHUNK], F32, name="y%d" % c)[:]
-            nc.vector.tensor_tensor(
-                y_tiles[c], acc[c][:], dc_rows[:, cols].unsqueeze(1).to_broadcast([P, PACK, CHUNK]), MULT
-            )
+            for b in range(2):
+                nc.vector.tensor_tensor(
+                    y_tiles[c][:, 2 * b : 2 * b + 2, :],
+                    acc[c, b][:],
+                    dc_rows[:, cols].unsqueeze(1).to_broadcast([P, 2, CHUNK]),
+                    MULT,
+                )
             if c == 1:
-                nc.sync.dma_start(out=y_rows[:, :, 0 : 2 * CHUNK], in_=y_pair[:])
+                nc.sync.dma_start(out=y_rows[:, :, 0:HALF], in_=y_pair[:])
             elif c > 1:
                 nc.sync.dma_start(out=y_rows[:, :, cols], in_=y_tiles[c])
-            y_bf[c] = sb.tile([P, CHUNK, PACK], BF16, name="y_bf%d" % c, align_bytes=64)
-            interleave(nc.vector.tensor_copy if c == CHUNKS - 1 else nc.scalar.copy, y_bf[c][:], y_tiles[c])
 
-        def planes(c):
-            quantize(y_codes, y_scales, slice(c * CHUNK, (c + 1) * CHUNK), y_bf[c])
-            if c % 2 == 1:
-                pair = slice((c - 1) * CHUNK, (c + 1) * CHUNK)
-                nc.sync.dma_start(out=word_rows[:, pair], in_=y_codes[:, pair].bitcast(I32))
+        def planes(h):
+            pair = slice(h * HALF, (h + 1) * HALF)
+            if h == 0:
+                quantize(y_codes, y_scales, pair, y_bf[h][:])
+            else:
+                for n in range(2):
+                    cols = slice(HALF + n * CHUNK, HALF + (n + 1) * CHUNK)
+                    quantize(y_codes, y_scales, cols, y_bf[h][:, n * CHUNK : (n + 1) * CHUNK, :])
+            nc.sync.dma_start(out=word_rows[:, pair], in_=y_codes[:, pair].bitcast(I32))
 
-        scores(0)
-        scores(1)
-        scores(2)
+        first_pass(0)
+        second_pass(0)
         decay(0)
-        scores(3)
+        first_pass(1)
         decay(1)
-        planes(0)
+        second_pass(1)
+        interleave(nc.scalar.copy, y_bf[0][:], y_pair[:])
         decay(2)
-        planes(1)
+        interleave(nc.scalar.copy, y_bf[1][:, 0:CHUNK, :], y_tiles[2])
         decay(3)
-        planes(2)
-        planes(3)
+        planes(0)
+        interleave(nc.vector.tensor_copy, y_bf[1][:, CHUNK:HALF, :], y_tiles[3])
+        planes(1)
         for quad in range(4):
             queue = nc.scalar if quad % 2 else nc.sync
             queue.dma_start(

@@ -40,7 +40,7 @@ def tile_attend_plw_decay_topk_kernel(tc, qT, k_words, k_scales, dc, offs, out_0
         nc.sync.dma_start(offsets[:], offs)
 
         scale_pool = sb.tile([P, POOL], U8, name="scale_pool")
-        nc.scalar.dma_start(
+        nc.sync.dma_start(
             out=scale_pool[0:32, :].bitcast(I32),
             in_=k_scales.rearrange("o f t -> f o t").bitcast(I32),
         )
@@ -48,16 +48,14 @@ def tile_attend_plw_decay_topk_kernel(tc, qT, k_words, k_scales, dc, offs, out_0
         nc.vector.memset(scale_pool[64:128, :].bitcast(I32), 0)
 
         dc_cols = sb.tile([P, PACK], F32, name="dc_cols")
-        nc.scalar.dma_start(out=dc_cols[:], in_=dc[0, 0].rearrange("(p m) -> p m", m=PACK))
+        nc.sync.dma_start(out=dc_cols[:], in_=dc[0, 0].rearrange("(p m) -> p m", m=PACK))
 
         word_pool = sb.tile([P, POOL], I32, name="word_pool")
         nc.sync.dma_start(out=word_pool[:], in_=k_words[0].rearrange("p t b -> p (t b)").bitcast(I32))
 
         q_rows = qT[0].rearrange("(o p j) q -> o p j q", o=PASSES, j=PACK)
-        raw = {}
-        for o in range(PASSES):
-            raw[0, o] = sb.tile([P, PACK, HALF], F32, name="raw0%d" % o)[:]
-            nc.sync.dma_start(out=raw[0, o], in_=q_rows[o][:, :, 0:HALF])
+        raw0 = sb.tile([P, PACK, NQ], F32, name="raw0")
+        nc.sync.dma_start(out=raw0[:], in_=q_rows[0])
 
         key_scales = sb.tile([P, PASSES, SLOTS], U8, name="key_scales", align_bytes=64)
         nc.vector.memset(key_scales[:].rearrange("p o s -> p (o s)").bitcast(I32), 0)
@@ -88,10 +86,9 @@ def tile_attend_plw_decay_topk_kernel(tc, qT, k_words, k_scales, dc, offs, out_0
                 in_=scales_dealt[8 * quad : 8 * quad + 8, :].bitcast(I32),
             )
 
-        raw_late = sb.tile([P, PASSES, PACK, HALF], F32, name="raw_late", tag="late")
-        for o in range(PASSES):
-            raw[1, o] = raw_late[:, o]
-            nc.sync.dma_start(out=raw[1, o], in_=q_rows[o][:, :, HALF:NQ])
+        raw1 = sb.tile([P, 2, PACK, HALF], F32, name="raw1", tag="late")
+        for h in range(2):
+            nc.sync.dma_start(out=raw1[:, h], in_=q_rows[1][:, :, h * HALF : (h + 1) * HALF])
 
         words_listed = sb.tile([P, SLOTS], U32, name="words_listed")
         nc.vector.tensor_copy(words_listed[:], word_pool[:].bitcast(U32).indirect(offsets[:]))
@@ -116,87 +113,73 @@ def tile_attend_plw_decay_topk_kernel(tc, qT, k_words, k_scales, dc, offs, out_0
         y_rows = out_0.rearrange("(s r) q -> s r q", r=PACK)
         word_rows = out_1[0].rearrange("p q b -> p (q b)").bitcast(I32)
 
-        acc = {}
-        y_tiles = [None] * CHUNKS
-        y_pair = sb.tile([P, PACK, HALF], F32, name="y_pair")
-        y_bf = [sb.tile([P, HALF, PACK], BF16, name="y_bf%d" % h, align_bytes=64) for h in range(2)]
+        def shared(dst, src, split):
+            interleave(nc.vector.tensor_copy, dst[:, 0:split, :], src[:, :, 0:split])
+            interleave(nc.scalar.copy, dst[:, split:, :], src[:, :, split:])
 
-        def one_pass(c, r, o):
-            cols = slice(c * CHUNK, (c + 1) * CHUNK)
-            nc.tensor.matmul_mx(
-                out=acc[c, r // 2][:, r % 2, :],
-                lhsT=key_words[:, o, 2 * P * r : 2 * P * (r + 1)].bitcast(FP4X4),
-                lhsT_scale=key_scales[:, o, P * r : P * (r + 1)],
-                rhs=q_codes[o][:, cols].bitcast(FP8X4),
-                rhs_scale=q_scales[o][:, cols],
-                start=(o == 0),
-                stop=(o == PASSES - 1),
-            )
+        acc = [psum.tile([P, NQ], F32, name="acc%d" % r) for r in range(PACK)]
 
-        def first_pass(h):
-            grouped = sb.tile([P, HALF, PACK], BF16, name="q0_bf%d" % h, align_bytes=64)
-            interleave(nc.scalar.copy, grouped[:], raw[h, 0])
-            quantize(q_codes[0], q_scales[0], slice(h * HALF, (h + 1) * HALF), grouped[:])
-            for c in (2 * h, 2 * h + 1):
-                for b in range(2):
-                    acc[c, b] = psum.tile([P, 2, CHUNK], F32, name="acc%d%d" % (c, b), tag="bank%d" % (2 * c + b))
-                    one_pass(c, 2 * b, 0)
-
-        def second_pass(h):
-            grouped = []
-            for n, copy in enumerate((nc.vector.tensor_copy, nc.scalar.copy)):
-                g = sb.tile([P, CHUNK, PACK], BF16, name="q1_bf%d%d" % (h, n), align_bytes=64)
-                interleave(copy, g[:], raw[h, 1][:, :, n * CHUNK : (n + 1) * CHUNK])
-                grouped.append(g)
-            for n in range(2):
-                c = 2 * h + n
-                quantize(q_codes[1], q_scales[1], slice(c * CHUNK, (c + 1) * CHUNK), grouped[n][:])
-                for b in range(2):
-                    one_pass(c, 2 * b, 1)
-                    one_pass(c, 2 * b + 1, 0)
-                    one_pass(c, 2 * b + 1, 1)
-
-        def decay(c):
-            cols = slice(c * CHUNK, (c + 1) * CHUNK)
-            if c < 2:
-                y_tiles[c] = y_pair[:, :, cols]
-            else:
-                y_tiles[c] = sb.tile([P, PACK, CHUNK], F32, name="y%d" % c)[:]
-            for b in range(2):
-                nc.vector.tensor_tensor(
-                    y_tiles[c][:, 2 * b : 2 * b + 2, :],
-                    acc[c, b][:],
-                    dc_rows[:, cols].unsqueeze(1).to_broadcast([P, 2, CHUNK]),
-                    MULT,
+        def passes(o):
+            for r in range(PACK):
+                nc.tensor.matmul_mx(
+                    out=acc[r][:],
+                    lhsT=key_words[:, o, 2 * P * r : 2 * P * (r + 1)].bitcast(FP4X4),
+                    lhsT_scale=key_scales[:, o, P * r : P * (r + 1)],
+                    rhs=q_codes[o][:].bitcast(FP8X4),
+                    rhs_scale=q_scales[o][:],
+                    start=(o == 0),
+                    stop=(o == PASSES - 1),
                 )
-            if c == 1:
-                nc.sync.dma_start(out=y_rows[:, :, 0:HALF], in_=y_pair[:])
-            elif c > 1:
-                nc.sync.dma_start(out=y_rows[:, :, cols], in_=y_tiles[c])
 
-        def planes(h):
-            pair = slice(h * HALF, (h + 1) * HALF)
-            if h == 0:
-                quantize(y_codes, y_scales, pair, y_bf[h][:])
-            else:
-                for n in range(2):
-                    cols = slice(HALF + n * CHUNK, HALF + (n + 1) * CHUNK)
-                    quantize(y_codes, y_scales, cols, y_bf[h][:, n * CHUNK : (n + 1) * CHUNK, :])
-            nc.sync.dma_start(out=word_rows[:, pair], in_=y_codes[:, pair].bitcast(I32))
+        q0_bf = sb.tile([P, NQ, PACK], BF16, name="q0_bf", align_bytes=64)
+        shared(q0_bf[:], raw0[:], 320)
+        quantize(q_codes[0], q_scales[0], slice(0, NQ), q0_bf[:])
+        passes(0)
+        q1_bf = [sb.tile([P, HALF, PACK], BF16, name="q1_bf%d" % h, align_bytes=64) for h in range(2)]
+        interleave(nc.vector.tensor_copy, q1_bf[0][:], raw1[:, 0])
+        quantize(q_codes[1], q_scales[1], slice(0, HALF), q1_bf[0][:])
+        shared(q1_bf[1][:], raw1[:, 1], 160)
+        quantize(q_codes[1], q_scales[1], slice(HALF, NQ), q1_bf[1][:])
+        passes(1)
 
-        first_pass(0)
-        second_pass(0)
-        decay(0)
-        first_pass(1)
-        decay(1)
-        second_pass(1)
-        interleave(nc.scalar.copy, y_bf[0][:], y_pair[:])
-        decay(2)
-        interleave(nc.scalar.copy, y_bf[1][:, 0:CHUNK, :], y_tiles[2])
-        decay(3)
+        y = sb.tile([P, PACK, NQ], F32, name="y")
+        y_bf = [sb.tile([P, CHUNK, PACK], BF16, name="y_bf%d" % c, align_bytes=64) for c in range(CHUNKS)]
+
+        def decay(r, cols):
+            nc.vector.tensor_tensor(y[:, r, cols], acc[r][:, cols], dc_rows[:, cols], MULT)
+
+        def chunk(c):
+            return slice(c * CHUNK, (c + 1) * CHUNK)
+
+        def round_y(c, copy):
+            interleave(copy, y_bf[c][:], y[:, :, chunk(c)])
+
+        def planes(c):
+            quantize(y_codes, y_scales, chunk(c), y_bf[c][:])
+
+        def store_words(cols):
+            nc.sync.dma_start(out=word_rows[:, cols], in_=y_codes[:, cols].bitcast(I32))
+
+        first, second = slice(0, HALF), slice(HALF, NQ)
+        decay(0, slice(0, NQ))
+        decay(1, slice(0, NQ))
+        nc.sync.dma_start(out=y_rows[:, 0:2, :], in_=y[:, 0:2, :])
+        for c in range(2):
+            decay(2, chunk(c))
+            decay(3, chunk(c))
+            round_y(c, nc.scalar.copy)
+        nc.sync.dma_start(out=y_rows[:, 2:4, first], in_=y[:, 2:4, first])
+        decay(2, second)
+        decay(3, second)
+        nc.sync.dma_start(out=y_rows[:, 2:4, second], in_=y[:, 2:4, second])
+        round_y(2, nc.scalar.copy)
         planes(0)
-        interleave(nc.vector.tensor_copy, y_bf[1][:, CHUNK:HALF, :], y_tiles[3])
+        round_y(3, nc.vector.tensor_copy)
         planes(1)
+        store_words(first)
+        planes(3)
+        planes(2)
+        store_words(second)
         for quad in range(4):
             queue = nc.scalar if quad % 2 else nc.sync
             queue.dma_start(

@@ -20,6 +20,7 @@ PASSES = 2
 CHUNK = 128
 CHUNKS = NQ // CHUNK
 HALF = 2 * CHUNK
+LAST = NQ - CHUNK
 FLOPS = 2 * SLOTS * D * NQ
 
 
@@ -48,11 +49,11 @@ def tile_attend_plw_decay_topk_kernel(tc, qT, k_words, k_scales, dc, offs, out_0
         nc.vector.memset(scale_pool[64:128, :].bitcast(I32), 0)
 
         dc_cols = sb.tile([P, PACK], F32, name="dc_cols")
-        nc.sync.dma_start(out=dc_cols[:], in_=dc[0, 0].rearrange("(p m) -> p m", m=PACK))
 
         word_pool = sb.tile([P, POOL], I32, name="word_pool")
         nc.sync.dma_start(out=word_pool[:], in_=k_words[0].rearrange("p t b -> p (t b)").bitcast(I32))
 
+        nc.sync.dma_start(out=dc_cols[:], in_=dc[0, 0].rearrange("(p m) -> p m", m=PACK))
         q_rows = qT[0].rearrange("(o p j) q -> o p j q", o=PASSES, j=PACK)
         raw0 = sb.tile([P, PACK, NQ], F32, name="raw0")
         nc.sync.dma_start(out=raw0[:], in_=q_rows[0])
@@ -60,7 +61,7 @@ def tile_attend_plw_decay_topk_kernel(tc, qT, k_words, k_scales, dc, offs, out_0
         key_scales = sb.tile([P, PASSES, SLOTS], U8, name="key_scales", align_bytes=64)
         nc.vector.memset(key_scales[:].rearrange("p o s -> p (o s)").bitcast(I32), 0)
 
-        ident = sb.tile([P, P], F32, name="ident")
+        ident = sb.tile([P, P], F32, name="ident", tag="early", align_bytes=64)
         ident_bf = sb.tile([P, P], BF16, name="ident_bf")
         make_identity(nc, ident_bf[:])
         nc.scalar.copy(out=ident[:], in_=ident_bf[:])
@@ -113,46 +114,67 @@ def tile_attend_plw_decay_topk_kernel(tc, qT, k_words, k_scales, dc, offs, out_0
         y_rows = out_0.rearrange("(s r) q -> s r q", r=PACK)
         word_rows = out_1[0].rearrange("p q b -> p (q b)").bitcast(I32)
 
-        def shared(dst, src, split):
-            interleave(nc.vector.tensor_copy, dst[:, 0:split, :], src[:, :, 0:split])
-            interleave(nc.scalar.copy, dst[:, split:, :], src[:, :, split:])
-
-        acc = [psum.tile([P, NQ], F32, name="acc%d" % r) for r in range(PACK)]
-
-        def passes(o):
-            for r in range(PACK):
-                nc.tensor.matmul_mx(
-                    out=acc[r][:],
-                    lhsT=key_words[:, o, 2 * P * r : 2 * P * (r + 1)].bitcast(FP4X4),
-                    lhsT_scale=key_scales[:, o, P * r : P * (r + 1)],
-                    rhs=q_codes[o][:].bitcast(FP8X4),
-                    rhs_scale=q_scales[o][:],
-                    start=(o == 0),
-                    stop=(o == PASSES - 1),
-                )
-
-        q0_bf = sb.tile([P, NQ, PACK], BF16, name="q0_bf", align_bytes=64)
-        shared(q0_bf[:], raw0[:], 320)
-        quantize(q_codes[0], q_scales[0], slice(0, NQ), q0_bf[:])
-        passes(0)
-        q1_bf = [sb.tile([P, HALF, PACK], BF16, name="q1_bf%d" % h, align_bytes=64) for h in range(2)]
-        interleave(nc.vector.tensor_copy, q1_bf[0][:], raw1[:, 0])
-        quantize(q_codes[1], q_scales[1], slice(0, HALF), q1_bf[0][:])
-        shared(q1_bf[1][:], raw1[:, 1], 160)
-        quantize(q_codes[1], q_scales[1], slice(HALF, NQ), q1_bf[1][:])
-        passes(1)
-
-        y = sb.tile([P, PACK, NQ], F32, name="y")
-        y_bf = [sb.tile([P, CHUNK, PACK], BF16, name="y_bf%d" % c, align_bytes=64) for c in range(CHUNKS)]
-
-        def decay(r, cols):
-            nc.vector.tensor_tensor(y[:, r, cols], acc[r][:, cols], dc_rows[:, cols], MULT)
-
         def chunk(c):
             return slice(c * CHUNK, (c + 1) * CHUNK)
 
+        acc = {}
+
+        def one_pass(c, r, o):
+            nc.tensor.matmul_mx(
+                out=acc[c, r // 2][:, r % 2, :],
+                lhsT=key_words[:, o, 2 * P * r : 2 * P * (r + 1)].bitcast(FP4X4),
+                lhsT_scale=key_scales[:, o, P * r : P * (r + 1)],
+                rhs=q_codes[o][:, chunk(c)].bitcast(FP8X4),
+                rhs_scale=q_scales[o][:, chunk(c)],
+                start=(o == 0),
+                stop=(o == PASSES - 1),
+            )
+
+        first, second = slice(0, HALF), slice(HALF, NQ)
+        q0_first = sb.tile([P, HALF, PACK], BF16, name="q0_first", tag="early", align_bytes=64)
+        q0_second = sb.tile([P, HALF, PACK], BF16, name="q0_second", align_bytes=64)
+        q1_bf = sb.tile([P, NQ, PACK], BF16, name="q1_bf", align_bytes=64)
+
+        def open_groups(c):
+            for b in range(2):
+                acc[c, b] = psum.tile([P, 2, CHUNK], F32, name="acc%d%d" % (c, b), tag="bank%d" % (2 * c + b))
+                one_pass(c, 2 * b, 0)
+
+        for c in range(2):
+            interleave(nc.scalar.copy, q0_first[:, chunk(c), :], raw0[:, :, chunk(c)])
+        interleave(nc.vector.tensor_copy, q0_second[:], raw0[:, :, second])
+        quantize(q_codes[0], q_scales[0], chunk(0), q0_first[:, chunk(0), :])
+        open_groups(0)
+        quantize(q_codes[0], q_scales[0], second, q0_second[:])
+        open_groups(2)
+        open_groups(3)
+        quantize(q_codes[0], q_scales[0], chunk(1), q0_first[:, chunk(1), :])
+        open_groups(1)
+
+        for c in range(CHUNKS):
+            copy = nc.vector.tensor_copy if c == 0 else nc.scalar.copy
+            interleave(copy, q1_bf[:, chunk(c), :], raw1[:, c // 2, :, chunk(c % 2)])
+        for c in range(CHUNKS):
+            quantize(q_codes[1], q_scales[1], chunk(c), q1_bf[:, chunk(c), :])
+            for b in range(2):
+                one_pass(c, 2 * b, 1)
+                one_pass(c, 2 * b + 1, 0)
+                one_pass(c, 2 * b + 1, 1)
+
+        y = [sb.tile([P, PACK, HALF], F32, name="y%d" % h) for h in range(2)]
+        y_bf = [sb.tile([P, CHUNK, PACK], BF16, name="y_bf%d" % c, align_bytes=64) for c in range(CHUNKS)]
+
+        def decay(c):
+            for b in range(2):
+                nc.vector.tensor_tensor(
+                    y[c // 2][:, 2 * b : 2 * b + 2, chunk(c % 2)],
+                    acc[c, b][:],
+                    dc_rows[:, chunk(c)].unsqueeze(1).to_broadcast([P, 2, CHUNK]),
+                    MULT,
+                )
+
         def round_y(c, copy):
-            interleave(copy, y_bf[c][:], y[:, :, chunk(c)])
+            interleave(copy, y_bf[c][:], y[c // 2][:, :, chunk(c % 2)])
 
         def planes(c):
             quantize(y_codes, y_scales, chunk(c), y_bf[c][:])
@@ -160,25 +182,20 @@ def tile_attend_plw_decay_topk_kernel(tc, qT, k_words, k_scales, dc, offs, out_0
         def store_words(cols):
             nc.sync.dma_start(out=word_rows[:, cols], in_=y_codes[:, cols].bitcast(I32))
 
-        first, second = slice(0, HALF), slice(HALF, NQ)
-        decay(0, slice(0, NQ))
-        decay(1, slice(0, NQ))
-        nc.sync.dma_start(out=y_rows[:, 0:2, :], in_=y[:, 0:2, :])
-        for c in range(2):
-            decay(2, chunk(c))
-            decay(3, chunk(c))
-            round_y(c, nc.scalar.copy)
-        nc.sync.dma_start(out=y_rows[:, 2:4, first], in_=y[:, 2:4, first])
-        decay(2, second)
-        decay(3, second)
-        nc.sync.dma_start(out=y_rows[:, 2:4, second], in_=y[:, 2:4, second])
-        round_y(2, nc.scalar.copy)
+        for c in range(CHUNKS):
+            decay(c)
+            if c == 1:
+                nc.sync.dma_start(out=y_rows[:, :, first], in_=y[0][:])
+            elif c > 1:
+                nc.sync.dma_start(out=y_rows[:, :, chunk(c)], in_=y[1][:, :, chunk(c % 2)])
+            if c < CHUNKS - 1:
+                round_y(c, nc.scalar.copy)
         planes(0)
-        round_y(3, nc.vector.tensor_copy)
+        round_y(CHUNKS - 1, nc.vector.tensor_copy)
         planes(1)
         store_words(first)
-        planes(3)
         planes(2)
+        planes(3)
         store_words(second)
         for quad in range(4):
             queue = nc.scalar if quad % 2 else nc.sync

@@ -16,19 +16,25 @@ MULT = mybir.AluOpType.mult
 P = 128
 PACK = 4
 SLOTS, POOL, D, NQ = 512, 2048, 1024, 512
-PASSES = 2
+PASSES = D // (P * PACK)
+QUADS = 4
 CHUNK = 128
 CHUNKS = NQ // CHUNK
 HALF = 2 * CHUNK
-LAST = NQ - CHUNK
+BANKS = 2
+RUN = 4
 FLOPS = 2 * SLOTS * D * NQ
 
 
 def interleave(copy, dst, src):
     copy(
-        out=dst.rearrange("p (c i) t -> p c t i", i=4),
-        in_=src.rearrange("p t (c i) -> p c t i", i=4),
+        out=dst.rearrange("p (c i) t -> p c t i", i=RUN),
+        in_=src.rearrange("p t (c i) -> p c t i", i=RUN),
     )
+
+
+def chunk(c):
+    return slice(c * CHUNK, (c + 1) * CHUNK)
 
 
 def tile_attend_plw_decay_topk_kernel(tc, qT, k_words, k_scales, dc, offs, out_0, out_1, out_2):
@@ -81,7 +87,7 @@ def tile_attend_plw_decay_topk_kernel(tc, qT, k_words, k_scales, dc, offs, out_0
             out=scales_dealt[:].rearrange("p (r s) -> p s r", r=PACK),
             in_=scales_listed[:].rearrange("p (s r) -> p s r", r=PACK),
         )
-        for quad in range(4):
+        for quad in range(QUADS):
             nc.sync.dma_start(
                 out=key_scales[32 * quad : 32 * quad + 4, :, :].bitcast(I32),
                 in_=scales_dealt[8 * quad : 8 * quad + 8, :].bitcast(I32),
@@ -114,9 +120,6 @@ def tile_attend_plw_decay_topk_kernel(tc, qT, k_words, k_scales, dc, offs, out_0
         y_rows = out_0.rearrange("(s r) q -> s r q", r=PACK)
         word_rows = out_1[0].rearrange("p q b -> p (q b)").bitcast(I32)
 
-        def chunk(c):
-            return slice(c * CHUNK, (c + 1) * CHUNK)
-
         acc = {}
 
         def one_pass(c, r, o):
@@ -136,8 +139,8 @@ def tile_attend_plw_decay_topk_kernel(tc, qT, k_words, k_scales, dc, offs, out_0
         q1_bf = sb.tile([P, NQ, PACK], BF16, name="q1_bf", align_bytes=64)
 
         def open_groups(c):
-            for b in range(2):
-                acc[c, b] = psum.tile([P, 2, CHUNK], F32, name="acc%d%d" % (c, b), tag="bank%d" % (2 * c + b))
+            for b in range(BANKS):
+                acc[c, b] = psum.tile([P, 2, CHUNK], F32, name="acc%d%d" % (c, b), tag="bank%d" % (BANKS * c + b))
                 one_pass(c, 2 * b, 0)
 
         for c in range(2):
@@ -156,27 +159,27 @@ def tile_attend_plw_decay_topk_kernel(tc, qT, k_words, k_scales, dc, offs, out_0
             interleave(copy, q1_bf[:, chunk(c), :], raw1[:, c // 2, :, chunk(c % 2)])
         for c in range(CHUNKS):
             quantize(q_codes[1], q_scales[1], chunk(c), q1_bf[:, chunk(c), :])
-            for b in range(2):
+            for b in range(BANKS):
                 one_pass(c, 2 * b, 1)
                 one_pass(c, 2 * b + 1, 0)
                 one_pass(c, 2 * b + 1, 1)
 
-        y = [sb.tile([P, PACK, HALF], F32, name="y%d" % h) for h in range(2)]
+        y = [sb.tile([P, PACK, CHUNK], F32, name="y%d" % c) for c in range(CHUNKS)]
         y_bf = [sb.tile([P, CHUNK, PACK], BF16, name="y_bf%d" % c, align_bytes=64) for c in range(CHUNKS)]
 
         def decay(c):
-            for b in range(2):
+            for b in range(BANKS):
                 nc.vector.tensor_tensor(
-                    y[c // 2][:, 2 * b : 2 * b + 2, chunk(c % 2)],
+                    y[c][:, 2 * b : 2 * b + 2, :],
                     acc[c, b][:],
                     dc_rows[:, chunk(c)].unsqueeze(1).to_broadcast([P, 2, CHUNK]),
                     MULT,
                 )
 
         def round_y(c, copy):
-            interleave(copy, y_bf[c][:], y[c // 2][:, :, chunk(c % 2)])
+            interleave(copy, y_bf[c][:], y[c][:])
 
-        def planes(c):
+        def quantize_y(c):
             quantize(y_codes, y_scales, chunk(c), y_bf[c][:])
 
         def store_words(cols):
@@ -184,20 +187,18 @@ def tile_attend_plw_decay_topk_kernel(tc, qT, k_words, k_scales, dc, offs, out_0
 
         for c in range(CHUNKS):
             decay(c)
-            if c == 1:
-                nc.sync.dma_start(out=y_rows[:, :, first], in_=y[0][:])
-            elif c > 1:
-                nc.sync.dma_start(out=y_rows[:, :, chunk(c)], in_=y[1][:, :, chunk(c % 2)])
+            nc.sync.dma_start(out=y_rows[:, :, chunk(c)], in_=y[c][:])
             if c < CHUNKS - 1:
                 round_y(c, nc.scalar.copy)
-        planes(0)
+        quantize_y(0)
         round_y(CHUNKS - 1, nc.vector.tensor_copy)
-        planes(1)
+        quantize_y(1)
         store_words(first)
-        planes(2)
-        planes(3)
+        quantize_y(2)
+        quantize_y(3)
         store_words(second)
-        for quad in range(4):
+
+        for quad in range(QUADS):
             queue = nc.scalar if quad % 2 else nc.sync
             queue.dma_start(
                 out=out_2[0, 4 * quad : 4 * quad + 4, :].bitcast(I32),

from contextlib import ExitStack

import concourse.mybir as mybir
from concourse.masks import make_identity

F32 = mybir.dt.float32
BF16 = mybir.dt.bfloat16
I32 = mybir.dt.int32
U32 = mybir.dt.uint32
U16 = mybir.dt.uint16
U8 = mybir.dt.uint8
FP8X4 = mybir.dt.float8_e4m3fn_x4
FP4X4 = mybir.dt.float4_e2m1fn_x4
MULT = mybir.AluOpType.mult

P = 128
PACK = 4
SLOTS, POOL, D, NQ = 512, 2048, 1024, 512
PASSES = D // (P * PACK)
QUADS = 4
CHUNK = 128
CHUNKS = NQ // CHUNK
HALF = 2 * CHUNK
BANKS = 2
RUN = 4
FLOPS = 2 * SLOTS * D * NQ


def interleave(copy, dst, src):
    copy(
        out=dst.rearrange("p (c i) t -> p c t i", i=RUN),
        in_=src.rearrange("p t (c i) -> p c t i", i=RUN),
    )


def chunk(c):
    return slice(c * CHUNK, (c + 1) * CHUNK)


def tile_attend_plw_decay_topk_kernel(tc, qT, k_words, k_scales, dc, offs, out_0, out_1, out_2):
    nc = tc.nc
    with ExitStack() as ctx:
        sb = ctx.enter_context(tc.tile_pool(name="sb", bufs=1))
        psum = ctx.enter_context(tc.psum_pool(name="psum", bufs=1))

        offsets = sb.tile([P, SLOTS // 16], U16, name="offsets")
        nc.sync.dma_start(offsets[:], offs)

        scale_pool = sb.tile([P, POOL], U8, name="scale_pool")
        nc.sync.dma_start(
            out=scale_pool[0:32, :].bitcast(I32),
            in_=k_scales.rearrange("o f t -> f o t").bitcast(I32),
        )
        nc.vector.memset(scale_pool[32:64, :].bitcast(I32), 0)
        nc.vector.memset(scale_pool[64:128, :].bitcast(I32), 0)

        dc_cols = sb.tile([P, PACK], F32, name="dc_cols")

        word_pool = sb.tile([P, POOL], I32, name="word_pool")
        nc.sync.dma_start(out=word_pool[:], in_=k_words[0].rearrange("p t b -> p (t b)").bitcast(I32))

        nc.sync.dma_start(out=dc_cols[:], in_=dc[0, 0].rearrange("(p m) -> p m", m=PACK))
        q_rows = qT[0].rearrange("(o p j) q -> o p j q", o=PASSES, j=PACK)
        raw0 = sb.tile([P, PACK, NQ], F32, name="raw0")
        nc.sync.dma_start(out=raw0[:], in_=q_rows[0])

        key_scales = sb.tile([P, PASSES, SLOTS], U8, name="key_scales", align_bytes=64)
        nc.vector.memset(key_scales[:].rearrange("p o s -> p (o s)").bitcast(I32), 0)

        ident = sb.tile([P, P], F32, name="ident", tag="early", align_bytes=64)
        ident_bf = sb.tile([P, P], BF16, name="ident_bf")
        make_identity(nc, ident_bf[:])
        nc.scalar.copy(out=ident[:], in_=ident_bf[:])
        dc_ps = psum.tile([P, PACK, P], F32, name="dc_ps", tag="bank7")
        for m in range(PACK):
            nc.tensor.transpose(dc_ps[:, m, :], dc_cols[:, m : m + 1].to_broadcast([P, P]), ident[:])
        dc_rows = sb.tile([P, NQ], F32, name="dc_rows")
        nc.scalar.copy(
            out=dc_rows[:].rearrange("p (n m) -> p n m", m=PACK),
            in_=dc_ps[:].rearrange("p m n -> p n m"),
        )

        scales_listed = sb.tile([P, SLOTS], U8, name="scales_listed", tag="late")
        nc.vector.tensor_copy(scales_listed[:], scale_pool[:].indirect(offsets[:]))
        scales_dealt = sb.tile([P, SLOTS], U8, name="scales_dealt")
        nc.vector.tensor_copy(
            out=scales_dealt[:].rearrange("p (r s) -> p s r", r=PACK),
            in_=scales_listed[:].rearrange("p (s r) -> p s r", r=PACK),
        )
        for quad in range(QUADS):
            nc.sync.dma_start(
                out=key_scales[32 * quad : 32 * quad + 4, :, :].bitcast(I32),
                in_=scales_dealt[8 * quad : 8 * quad + 8, :].bitcast(I32),
            )

        raw1 = sb.tile([P, 2, PACK, HALF], F32, name="raw1", tag="late")
        for h in range(2):
            nc.sync.dma_start(out=raw1[:, h], in_=q_rows[1][:, :, h * HALF : (h + 1) * HALF])

        words_listed = sb.tile([P, SLOTS], U32, name="words_listed")
        nc.vector.tensor_copy(words_listed[:], word_pool[:].bitcast(U32).indirect(offsets[:]))
        key_words = sb.tile([P, PASSES, 2 * SLOTS], U8, name="key_words", align_bytes=64)
        nc.vector.tensor_copy(
            out=key_words[:].bitcast(U16).rearrange("p o (r s) -> p o s r", r=PACK),
            in_=words_listed[:].bitcast(U16).rearrange("p (s r o) -> p o s r", r=PACK, o=PASSES),
        )

        q_codes = [sb.tile([P, NQ], U32, name="q_codes%d" % o, align_bytes=64) for o in range(PASSES)]
        q_scales = [sb.tile([P, NQ], U8, name="q_scales%d" % o, align_bytes=64) for o in range(PASSES)]

        def quantize(codes, scales, cols, grouped):
            nc.vector.quantize_mx(
                out=codes[:, cols].bitcast(FP8X4),
                scales=scales[:, cols],
                in_=grouped.rearrange("p c t -> p (c t)"),
            )

        y_codes = sb.tile([P, NQ], U32, name="y_codes", align_bytes=64)
        y_scales = sb.tile([P, NQ], U8, name="y_scales", align_bytes=64)
        y_rows = out_0.rearrange("(s r) q -> s r q", r=PACK)
        word_rows = out_1[0].rearrange("p q b -> p (q b)").bitcast(I32)

        acc = {}

        def one_pass(c, r, o):
            nc.tensor.matmul_mx(
                out=acc[c, r // 2][:, r % 2, :],
                lhsT=key_words[:, o, 2 * P * r : 2 * P * (r + 1)].bitcast(FP4X4),
                lhsT_scale=key_scales[:, o, P * r : P * (r + 1)],
                rhs=q_codes[o][:, chunk(c)].bitcast(FP8X4),
                rhs_scale=q_scales[o][:, chunk(c)],
                start=(o == 0),
                stop=(o == PASSES - 1),
            )

        first, second = slice(0, HALF), slice(HALF, NQ)
        q0_first = sb.tile([P, HALF, PACK], BF16, name="q0_first", tag="early", align_bytes=64)
        q0_second = sb.tile([P, HALF, PACK], BF16, name="q0_second", align_bytes=64)
        q1_bf = sb.tile([P, NQ, PACK], BF16, name="q1_bf", align_bytes=64)

        def open_groups(c):
            for b in range(BANKS):
                acc[c, b] = psum.tile([P, 2, CHUNK], F32, name="acc%d%d" % (c, b), tag="bank%d" % (BANKS * c + b))
                one_pass(c, 2 * b, 0)

        for c in range(2):
            interleave(nc.scalar.copy, q0_first[:, chunk(c), :], raw0[:, :, chunk(c)])
        interleave(nc.vector.tensor_copy, q0_second[:], raw0[:, :, second])
        quantize(q_codes[0], q_scales[0], chunk(0), q0_first[:, chunk(0), :])
        open_groups(0)
        quantize(q_codes[0], q_scales[0], second, q0_second[:])
        open_groups(2)
        open_groups(3)
        quantize(q_codes[0], q_scales[0], chunk(1), q0_first[:, chunk(1), :])
        open_groups(1)

        for c in range(CHUNKS):
            copy = nc.vector.tensor_copy if c == 0 else nc.scalar.copy
            interleave(copy, q1_bf[:, chunk(c), :], raw1[:, c // 2, :, chunk(c % 2)])
        for c in range(CHUNKS):
            quantize(q_codes[1], q_scales[1], chunk(c), q1_bf[:, chunk(c), :])
            for b in range(BANKS):
                one_pass(c, 2 * b, 1)
                one_pass(c, 2 * b + 1, 0)
                one_pass(c, 2 * b + 1, 1)

        y = [sb.tile([P, PACK, CHUNK], F32, name="y%d" % c) for c in range(CHUNKS)]
        y_bf = [sb.tile([P, CHUNK, PACK], BF16, name="y_bf%d" % c, align_bytes=64) for c in range(CHUNKS)]

        def decay(c):
            for b in range(BANKS):
                nc.vector.tensor_tensor(
                    y[c][:, 2 * b : 2 * b + 2, :],
                    acc[c, b][:],
                    dc_rows[:, chunk(c)].unsqueeze(1).to_broadcast([P, 2, CHUNK]),
                    MULT,
                )

        def round_y(c, copy):
            interleave(copy, y_bf[c][:], y[c][:])

        def quantize_y(c):
            quantize(y_codes, y_scales, chunk(c), y_bf[c][:])

        def store_words(cols):
            nc.sync.dma_start(out=word_rows[:, cols], in_=y_codes[:, cols].bitcast(I32))

        for c in range(CHUNKS):
            decay(c)
            nc.sync.dma_start(out=y_rows[:, :, chunk(c)], in_=y[c][:])
            if c < CHUNKS - 1:
                round_y(c, nc.scalar.copy)
        quantize_y(0)
        round_y(CHUNKS - 1, nc.vector.tensor_copy)
        quantize_y(1)
        store_words(first)
        quantize_y(2)
        quantize_y(3)
        store_words(second)

        for quad in range(QUADS):
            queue = nc.scalar if quad % 2 else nc.sync
            queue.dma_start(
                out=out_2[0, 4 * quad : 4 * quad + 4, :].bitcast(I32),
                in_=y_scales[32 * quad : 32 * quad + 4, :].bitcast(I32),
            )
